import numpy as np
import ml_dtypes


def mxq(x, axis, fmt="e4m3"):
    dtype, down = {"e4m3": (ml_dtypes.float8_e4m3fn, 7), "e5m2": (ml_dtypes.float8_e5m2, 14)}[fmt]
    v = np.moveaxis(np.asarray(x, np.float32).astype(ml_dtypes.bfloat16).astype(np.float64), axis, -1)
    blocks = v.reshape(v.shape[:-1] + (-1, 32))
    amax = np.abs(blocks).max(-1, keepdims=True)
    byte = np.maximum(np.where(amax > 0, np.frexp(amax)[1] - 1 + 127, 0) - down, 1)
    scale = np.exp2(byte - 127.0)
    codes = (blocks / scale).astype(np.float32).astype(dtype).astype(np.float64)
    return np.moveaxis((codes * scale).reshape(v.shape), -1, axis)


WIDE = False


def mx_kscale(k):
    if not WIDE:
        return np.ones(k)
    levels = np.array([10, -10, 5, -5, 0])
    if k % 512:
        return np.exp2(np.random.permutation(np.resize(levels, k // 32))).repeat(32)
    a = np.empty((k // 512, 16))
    for p in range(k // 512):
        a[p, :8] = np.random.permutation(np.resize(levels, 8))
        for g in range(8):
            far = levels[np.abs(levels - a[p, g]) >= 10]
            a[p, g + 8] = far[np.random.randint(len(far))]
    return np.exp2(a.ravel()).repeat(32)


BF16 = ml_dtypes.bfloat16


def bf(x):
    return np.asarray(x, np.float32).astype(BF16)


def f64(x):
    return np.asarray(x).astype(np.float64)


N, F, S, B = 2048, 1024, 1024, 1024

CAP = 2.0


def draw0():
    s = mx_kscale(F)
    t = mx_kscale(N)
    sens = np.random.standard_normal((N, F)) / np.sqrt(F)
    shocks = np.random.standard_normal((F, S))
    tilt = 0.5 * np.random.standard_normal(N)
    cap = CAP * (1 + 0.1 * np.random.standard_normal(N))
    short = np.random.standard_normal((B, N)) / np.sqrt(N)
    return {"sens": bf(sens * s * t[:, None]),
            "shocks": bf(shocks / s[:, None]),
            "tilt": bf(tilt * t),
            "cap": bf(cap * t * t),
            "short": bf(short / (t * t))}


def core(sens, shocks, tilt, cap, short):
    y = mxq(f64(sens), 1, "e4m3") @ mxq(f64(shocks), 0, "e4m3")
    v = y * (y + f64(tilt)[:, None])
    v = np.minimum(v, f64(cap)[:, None])
    loss = mxq(f64(short), 1, "e4m3") @ mxq(v, 0, "e4m3")
    return loss


def e4m3fn_bytes(y):
    return np.clip(np.asarray(y, np.float64), -448.0, 448.0).astype(np.float32).astype(ml_dtypes.float8_e4m3fn).view(np.uint8)


def e4m3fn_values(b):
    return np.asarray(b, np.uint8).view(ml_dtypes.float8_e4m3fn).astype(np.float64)


def setup_inputs():
    d = draw0()
    x0 = np.asarray(d['short']).astype(np.float64)
    s = (np.max(np.abs(x0), axis=(0,), keepdims=True) / 448.0).astype(np.float32)
    out = {}
    for k, v in d.items():
        if k == 'short':
            out['short_bytes'] = e4m3fn_bytes(x0 / s.astype(np.float64))
            out['short_scale'] = s
        else:
            out[k] = v
    return out


def reference(sens, shocks, tilt, cap, short_bytes, short_scale):
    return core(sens, shocks, tilt, cap, e4m3fn_values(short_bytes) * short_scale.astype(np.float64))

@@ -1,0 +1,330 @@
+from contextlib import ExitStack
+
+import concourse.mybir as mybir
+from concourse.masks import make_identity
+
+N, F, S, B = 2048, 1024, 1024, 1024
+FLOPS = 2 * N * F * S + 2 * B * N * S
+
+F32 = mybir.dt.float32
+BF16 = mybir.dt.bfloat16
+U32 = mybir.dt.uint32
+U8 = mybir.dt.uint8
+FP8 = mybir.dt.float8_e4m3fn
+X4 = mybir.dt.float8_e4m3fn_x4
+ALU = mybir.AluOpType
+ACT = mybir.ActivationFunctionType
+
+P = 128
+T = 4
+KP = P * T
+GF = F // KP
+GN = N // KP
+H = 512
+NB = B // P
+
+
+def tile_scenario_delta_gamma_losses_s7_kernel(tc, sens, shocks, tilt, cap, short_bytes, short_scale, out):
+    nc = tc.nc
+    with ExitStack() as ctx:
+        keep = ctx.enter_context(tc.tile_pool(name="keep", bufs=1))
+        work = ctx.enter_context(tc.tile_pool(name="work", bufs=2))
+        psum = ctx.enter_context(tc.psum_pool(name="psum", bufs=3))
+
+        warm = keep.tile([P, 1], F32, name="warm")
+        nc.vector.memset(warm[:], 0.0)
+        nc.scalar.activation(out=warm[:], in_=warm[:], func=ACT.Square)
+        ident = keep.tile([P, P], F32, name="ident")
+        make_identity(nc, ident[:])
+
+        tilt_bf = keep.tile([P, GN, 16], BF16, name="tilt_bf")
+        cap_bf = keep.tile([P, GN, 16], BF16, name="cap_bf")
+        nc.scalar.dma_start(out=tilt_bf[:, :, 0:T], in_=tilt.rearrange("(g p t) -> p g t", p=P, t=T))
+        nc.scalar.dma_start(out=cap_bf[:, :, 0:T], in_=cap.rearrange("(g p t) -> p g t", p=P, t=T))
+
+        half_tilt = keep.tile([P, GN, T], F32, name="half_tilt")
+        quarter_sq = keep.tile([P, GN, T], F32, name="quarter_sq")
+        cap_f = keep.tile([P, GN, T], F32, name="cap_f")
+
+        def small_constants():
+            nc.vector.tensor_scalar(out=half_tilt[:], in0=tilt_bf[:, :, 0:T], scalar1=0.5, scalar2=None, op0=ALU.mult)
+            nc.vector.tensor_copy(out=cap_f[:], in_=cap_bf[:, :, 0:T])
+            nc.vector.tensor_tensor(out=quarter_sq[:], in0=half_tilt[:], in1=half_tilt[:], op=ALU.mult)
+
+        sens_v = sens.rearrange("(g m t) k -> g m t k", m=P, t=T)
+        shocks_v = shocks.rearrange("(g p t) s -> g p t s", p=P, t=T)
+        sens_raw = {}
+        shocks_raw = {}
+
+        def load_sens(g, t0, n):
+            raw = keep.tile([P, n, F], BF16, name="sens_raw_%d_%d" % (g, t0))
+            nc.sync.dma_start(out=raw[:], in_=sens_v[g][:, t0 : t0 + n, :])
+            for t in range(n):
+                sens_raw[(g, t0 + t)] = raw[:, t, :]
+
+        def load_shocks(g, h):
+            raw = keep.tile([P, T, H], BF16, name="shocks_raw_%d_%d" % (g, h))
+            nc.sync.dma_start(out=raw[:], in_=shocks_v[g][:, :, h * H : (h + 1) * H])
+            shocks_raw[(g, h)] = raw
+
+        load_sens(0, 0, 2)
+        load_shocks(0, 0)
+        load_shocks(1, 0)
+        load_sens(0, 2, 2)
+        load_shocks(0, 1)
+        load_shocks(1, 1)
+        load_sens(1, 0, 4)
+        load_sens(2, 0, 4)
+        bytes_t = keep.tile([P, NB, N], U8, name="bytes_t")
+        scale_t = keep.tile([P, N], F32, name="scale_t")
+        bytes_v = short_bytes.rearrange("(i p) k -> p i k", p=P)
+        nc.sync.dma_start(out=scale_t[:], in_=short_scale.rearrange("o k -> (o k)").partition_broadcast(P))
+        nc.sync.dma_start(out=bytes_t[:, 0:2, :], in_=bytes_v[:, 0:2, :])
+        load_sens(3, 0, 4)
+        nc.sync.dma_start(out=bytes_t[:, 2:5, :], in_=bytes_v[:, 2:5, :])
+        nc.sync.dma_start(out=bytes_t[:, 5:8, :], in_=bytes_v[:, 5:8, :])
+
+        sh_codes = keep.tile([P, GF, S], U32, name="sh_codes", align_bytes=64)
+        sh_scales = keep.tile([P, GF, S], U8, name="sh_scales", align_bytes=64)
+        v_codes = [keep.tile([P, S], U32, name="v_codes_%d" % g, align_bytes=64) for g in range(GN)]
+        v_scales = [keep.tile([P, S], U8, name="v_scales_%d" % g, align_bytes=64) for g in range(GN)]
+
+        sh_grouped = {}
+
+        def shocks_interleave(g, h, on_vector):
+            grouped = work.tile([P, H, T], BF16, name="sh_grouped", align_bytes=64)
+            src = shocks_raw[(g, h)][:].rearrange("p t n -> p n t")
+            c = on_vector
+            if c > 0:
+                nc.vector.tensor_copy(out=grouped[:, 0:c, :], in_=src[:, 0:c, :])
+            if c < H:
+                nc.scalar.copy(out=grouped[:, c:H, :], in_=src[:, c:H, :])
+            sh_grouped[(g, h)] = grouped
+
+        def shocks_quantise(g, h):
+            cols = slice(h * H, (h + 1) * H)
+            nc.vector.quantize_mx(out=sh_codes[:, g, cols].bitcast(X4), scales=sh_scales[:, g, cols],
+                                  in_=sh_grouped[(g, h)][:].rearrange("p n t -> p (n t)"))
+
+        sens_bank = {}
+        sens_grouped = {}
+        sens_codes = {}
+
+        def sens_transpose(g, t):
+            bank = psum.tile([P, GF, 2, P], F32, name="tr")
+            words = sens_raw[(g, t)].bitcast(F32)
+            for q in range(GF):
+                for u in range(2):
+                    nc.tensor.transpose(bank[:, q, u, :], words[:, 256 * q + u : 256 * (q + 1) : 2], ident[:])
+            sens_bank[(g, t)] = bank
+
+        def sens_copy(g, t):
+            if t % 2 == 0:
+                sens_grouped[(g, t // 2)] = work.tile([P, 2, GF, P, T], BF16, name="sens_grouped", align_bytes=64)
+            dst = sens_grouped[(g, t // 2)][:, t % 2].rearrange("p q m j -> p (q m j)").bitcast(F32)
+            nc.scalar.copy(out=dst.rearrange("p (q m u) -> p q m u", q=GF, u=2),
+                           in_=sens_bank[(g, t)][:].rearrange("p q u m -> p q m u"))
+
+        def sens_quantise(g, half):
+            codes = work.tile([P, 2, GF, P], U32, name="sens_codes", align_bytes=64, bufs=8)
+            scales = work.tile([P, 2, GF, P], U8, name="sens_scales", align_bytes=64, bufs=8)
+            nc.vector.quantize_mx(out=codes[:].rearrange("p a q m -> p (a q m)").bitcast(X4),
+                                  scales=scales[:].rearrange("p a q m -> p (a q m)"),
+                                  in_=sens_grouped[(g, half)][:].rearrange("p a q m j -> p (a q m j)"))
+            sens_codes[(g, half)] = (codes, scales)
+
+        v_sq = {}
+        v_flat = {}
+        v_grouped = {}
+        y_bank = {}
+
+        def y_product(g, t, h):
+            codes, scales = sens_codes[(g, t // 2)]
+            cols = slice(h * H, (h + 1) * H)
+            bank = psum.tile([P, H], F32, name="acc", bufs=5)
+            for q in range(GF):
+                nc.tensor.matmul_mx(out=bank[:], lhsT=codes[:, t % 2, q, :].bitcast(X4), lhsT_scale=scales[:, t % 2, q, :],
+                                    rhs=sh_codes[:, q, cols].bitcast(X4), rhs_scale=sh_scales[:, q, cols],
+                                    start=(q == 0), stop=(q == GF - 1))
+            y_bank[(g, t, h)] = bank
+
+        def y_square(g, t, h):
+            if (g, t) not in v_sq:
+                v_sq[(g, t)] = work.tile([P, S], F32, name="v_sq", bufs=5)
+            nc.scalar.activation(out=v_sq[(g, t)][:, h * H : (h + 1) * H], in_=y_bank[(g, t, h)][:], func=ACT.Square,
+                                 bias=half_tilt[:, g, t : t + 1])
+
+        def v_clip(g, t, h, n):
+            if g not in v_flat:
+                v_flat[g] = work.tile([P, T, S], BF16, name="v_flat", bufs=2)
+            cols = slice(h * H, (h + n) * H)
+            nc.vector.tensor_scalar(out=v_flat[g][:, t, cols], in0=v_sq[(g, t)][:, cols],
+                                    scalar1=quarter_sq[:, g, t : t + 1], scalar2=cap_f[:, g, t : t + 1],
+                                    op0=ALU.subtract, op1=ALU.min)
+
+        def v_interleave(g, h, on_vector):
+            grouped = work.tile([P, H, T], BF16, name="v_grouped", align_bytes=64, bufs=3)
+            src = v_flat[g][:, :, h * H : (h + 1) * H].rearrange("p t n -> p n t")
+            c = on_vector
+            if c > 0:
+                nc.vector.tensor_copy(out=grouped[:, 0:c, :], in_=src[:, 0:c, :])
+            if c < H:
+                nc.scalar.copy(out=grouped[:, c:H, :], in_=src[:, c:H, :])
+            v_grouped[(g, h)] = grouped
+
+        def v_quantise(g, h):
+            cols = slice(h * H, (h + 1) * H)
+            nc.vector.quantize_mx(out=v_codes[g][:, cols].bitcast(X4), scales=v_scales[g][:, cols],
+                                  in_=v_grouped[(g, h)][:].rearrange("p n t -> p (n t)"))
+
+        st_wide = {}
+        st_bank = {}
+        st_grouped = {}
+        st_codes = {}
+
+        def short_widen(i):
+            wide = work.tile([P, N], BF16, name="st_wide", bufs=3)
+            nc.vector.tensor_tensor(out=wide[:], in0=bytes_t[:, i, :].bitcast(FP8), in1=scale_t[:], op=ALU.mult)
+            st_wide[i] = wide
+
+        def short_transpose(i, half):
+            bank = psum.tile([P, 2, 2, P], F32, name="tr")
+            words = st_wide[i][:].bitcast(F32)
+            for q in range(2):
+                for u in range(2):
+                    k0 = 256 * (2 * half + q)
+                    nc.tensor.transpose(bank[:, q, u, :], words[:, k0 + u : k0 + 256 : 2], ident[:])
+            st_bank[(i, half)] = bank
+
+        def short_copy(i, half):
+            if half == 0:
+                st_grouped[i] = work.tile([P, GN, P, T], BF16, name="st_grouped", align_bytes=64)
+            dst = st_grouped[i][:, 2 * half : 2 * half + 2].rearrange("p q m j -> p (q m j)").bitcast(F32)
+            nc.scalar.copy(out=dst.rearrange("p (q m u) -> p q m u", q=2, u=2),
+                           in_=st_bank[(i, half)][:].rearrange("p q u m -> p q m u"))
+
+        def short_quantise(i):
+            codes = work.tile([P, GN, P], U32, name="st_codes", align_bytes=64, bufs=3)
+            scales = work.tile([P, GN, P], U8, name="st_scales", align_bytes=64, bufs=3)
+            nc.vector.quantize_mx(out=codes[:].rearrange("p q m -> p (q m)").bitcast(X4),
+                                  scales=scales[:].rearrange("p q m -> p (q m)"),
+                                  in_=st_grouped[i][:].rearrange("p q m j -> p (q m j)"))
+            st_codes[i] = (codes, scales)
+
+        l_bank = {}
+        l_out = {}
+
+        def loss_product(i, h, g0, g1):
+            codes, scales = st_codes[i]
+            cols = slice(h * H, (h + 1) * H)
+            if g0 == 0:
+                l_bank[(i, h)] = psum.tile([P, H], F32, name="acc", bufs=5)
+            for g in range(g0, g1):
+                nc.tensor.matmul_mx(out=l_bank[(i, h)][:], lhsT=codes[:, g, :].bitcast(X4), lhsT_scale=scales[:, g, :],
+                                    rhs=v_codes[g][:, cols].bitcast(X4), rhs_scale=v_scales[g][:, cols],
+                                    start=(g == 0), stop=(g == GN - 1))
+
+        def loss_copy(i, h, on_vector):
+            if h == 0:
+                l_out[i] = work.tile([P, S], F32, name="l_out", bufs=3)
+            dst = l_out[i][:, h * H : (h + 1) * H]
+            if on_vector:
+                nc.vector.tensor_copy(out=dst, in_=l_bank[(i, h)][:])
+            else:
+                nc.scalar.copy(out=dst, in_=l_bank[(i, h)][:])
+
+        def loss_store(i):
+            nc.sync.dma_start(out=out[i * P : (i + 1) * P, :], in_=l_out[i][:])
+
+        def sens_half(g, a):
+            for t in (2 * a, 2 * a + 1):
+                sens_transpose(g, t)
+                sens_copy(g, t)
+            sens_quantise(g, a)
+
+        def shocks_all(g, h, c):
+            shocks_interleave(g, h, c)
+            shocks_quantise(g, h)
+
+        def vq(g, h, c):
+            v_interleave(g, h, c)
+            v_quantise(g, h)
+
+        def ys(g, h):
+            for t in range(T):
+                y_product(g, t, h)
+                y_square(g, t, h)
+                v_clip(g, t, h, 1)
+
+        def yw(g):
+            for t in range(T):
+                for h in range(2):
+                    y_product(g, t, h)
+                    y_square(g, t, h)
+                v_clip(g, t, 0, 2)
+
+        def short_rest(i):
+            short_transpose(i, 0)
+            short_copy(i, 0)
+            short_transpose(i, 1)
+            short_copy(i, 1)
+            short_quantise(i)
+
+        def loss_early(i, h):
+            loss_product(i, h, 0, 3)
+
+        def loss_late(i, h, on_vector):
+            loss_product(i, h, 3, 4)
+            loss_copy(i, h, on_vector)
+
+        def loss(i, h, on_vector):
+            loss_product(i, h, 0, 4)
+            loss_copy(i, h, on_vector)
+
+        sens_half(0,0)
+        shocks_all(0,0,512)
+        shocks_all(1,0,384)
+        small_constants()
+        sens_half(0,1)
+        ys(0,0)
+        sens_half(1,0)
+        shocks_all(0,1,320)
+        shocks_all(1,1,256)
+        vq(0,0,512)
+        ys(0,1)
+        sens_half(1,1)
+        vq(0,1,512)
+        yw(1)
+        sens_half(2,0)
+        vq(1,0,448)
+        sens_half(2,1)
+        vq(1,1,448)
+        yw(2)
+        sens_half(3,0)
+        vq(2,0,448)
+        sens_half(3,1)
+        vq(2,1,448)
+        yw(3)
+        vq(3,0,384)
+        vq(3,1,320)
+        short_widen(0)
+        short_rest(0)
+        short_widen(1)
+        short_rest(1)
+        for i in range(2):
+            for h in range(2):
+                loss_early(i,h)
+        for i in range(2):
+            for h in range(2):
+                loss_late(i,h,False)
+            loss_store(i)
+        short_widen(2)
+        short_rest(2)
+        for i in range(2,NB):
+            if i+1<NB:
+                short_widen(i+1)
+            loss(i,0,False)
+            if i+1<NB:
+                short_rest(i+1)
+            loss(i,1,i==NB-1)
+            loss_store(i)

@@ -22,6 +22,7 @@ GF = F // KP
 GN = N // KP
 H = 512
 NB = B // P
+WIDE = (1, 2)
 
 
 def tile_scenario_delta_gamma_losses_s7_kernel(tc, sens, shocks, tilt, cap, short_bytes, short_scale, out):
@@ -67,22 +68,24 @@ def tile_scenario_delta_gamma_losses_s7_kernel(tc, sens, shocks, tilt, cap, shor
             nc.sync.dma_start(out=raw[:], in_=shocks_v[g][:, :, h * H : (h + 1) * H])
             shocks_raw[(g, h)] = raw
 
-        load_sens(0, 0, 2)
         load_shocks(0, 0)
+        load_sens(0, 0, 2)
         load_shocks(1, 0)
         load_sens(0, 2, 2)
         load_shocks(0, 1)
         load_shocks(1, 1)
         load_sens(1, 0, 4)
-        load_sens(2, 0, 4)
         bytes_t = keep.tile([P, NB, N], U8, name="bytes_t")
         scale_t = keep.tile([P, N], F32, name="scale_t")
         bytes_v = short_bytes.rearrange("(i p) k -> p i k", p=P)
+        load_sens(2, 0, 4)
         nc.sync.dma_start(out=scale_t[:], in_=short_scale.rearrange("o k -> (o k)").partition_broadcast(P))
         nc.sync.dma_start(out=bytes_t[:, 0:2, :], in_=bytes_v[:, 0:2, :])
         load_sens(3, 0, 4)
         nc.sync.dma_start(out=bytes_t[:, 2:5, :], in_=bytes_v[:, 2:5, :])
         nc.sync.dma_start(out=bytes_t[:, 5:8, :], in_=bytes_v[:, 5:8, :])
+
+        ctx.enter_context(tc.manual_schedule())
 
         sh_codes = keep.tile([P, GF, S], U32, name="sh_codes", align_bytes=64)
         sh_scales = keep.tile([P, GF, S], U8, name="sh_scales", align_bytes=64)
@@ -93,12 +96,13 @@ def tile_scenario_delta_gamma_losses_s7_kernel(tc, sens, shocks, tilt, cap, shor
 
         def shocks_interleave(g, h, on_vector):
             grouped = work.tile([P, H, T], BF16, name="sh_grouped", align_bytes=64)
-            src = shocks_raw[(g, h)][:].rearrange("p t n -> p n t")
-            c = on_vector
+            src = shocks_raw[(g, h)][:].rearrange("p t (b c) -> p b t c", c=4)
+            dst = grouped[:].rearrange("p (b c) t -> p b t c", c=4)
+            c = on_vector // 4
             if c > 0:
-                nc.vector.tensor_copy(out=grouped[:, 0:c, :], in_=src[:, 0:c, :])
-            if c < H:
-                nc.scalar.copy(out=grouped[:, c:H, :], in_=src[:, c:H, :])
+                nc.vector.tensor_copy(out=dst[:, 0:c], in_=src[:, 0:c])
+            if c < H // 4:
+                nc.scalar.copy(out=dst[:, c:], in_=src[:, c:])
             sh_grouped[(g, h)] = grouped
 
         def shocks_quantise(g, h):
@@ -164,12 +168,13 @@ def tile_scenario_delta_gamma_losses_s7_kernel(tc, sens, shocks, tilt, cap, shor
 
         def v_interleave(g, h, on_vector):
             grouped = work.tile([P, H, T], BF16, name="v_grouped", align_bytes=64, bufs=3)
-            src = v_flat[g][:, :, h * H : (h + 1) * H].rearrange("p t n -> p n t")
-            c = on_vector
+            src = v_flat[g][:, :, h * H : (h + 1) * H].rearrange("p t (b c) -> p b t c", c=4)
+            dst = grouped[:].rearrange("p (b c) t -> p b t c", c=4)
+            c = on_vector // 4
             if c > 0:
-                nc.vector.tensor_copy(out=grouped[:, 0:c, :], in_=src[:, 0:c, :])
-            if c < H:
-                nc.scalar.copy(out=grouped[:, c:H, :], in_=src[:, c:H, :])
+                nc.vector.tensor_copy(out=dst[:, 0:c], in_=src[:, 0:c])
+            if c < H // 4:
+                nc.scalar.copy(out=dst[:, c:], in_=src[:, c:])
             v_grouped[(g, h)] = grouped
 
         def v_quantise(g, h):
@@ -214,18 +219,18 @@ def tile_scenario_delta_gamma_losses_s7_kernel(tc, sens, shocks, tilt, cap, shor
         l_bank = {}
         l_out = {}
 
-        def loss_product(i, h, g0, g1):
+        def loss_product(i, h, g0, n):
             codes, scales = st_codes[i]
             cols = slice(h * H, (h + 1) * H)
             if g0 == 0:
                 l_bank[(i, h)] = psum.tile([P, H], F32, name="acc", bufs=5)
-            for g in range(g0, g1):
+            for g in range(g0, g0 + n):
                 nc.tensor.matmul_mx(out=l_bank[(i, h)][:], lhsT=codes[:, g, :].bitcast(X4), lhsT_scale=scales[:, g, :],
                                     rhs=v_codes[g][:, cols].bitcast(X4), rhs_scale=v_scales[g][:, cols],
                                     start=(g == 0), stop=(g == GN - 1))
 
         def loss_copy(i, h, on_vector):
-            if h == 0:
+            if i not in l_out:
                 l_out[i] = work.tile([P, S], F32, name="l_out", bufs=3)
             dst = l_out[i][:, h * H : (h + 1) * H]
             if on_vector:
@@ -233,98 +238,103 @@ def tile_scenario_delta_gamma_losses_s7_kernel(tc, sens, shocks, tilt, cap, shor
             else:
                 nc.scalar.copy(out=dst, in_=l_bank[(i, h)][:])
 
-        def loss_store(i):
-            nc.sync.dma_start(out=out[i * P : (i + 1) * P, :], in_=l_out[i][:])
+        def loss_store(i, h, n):
+            cols = slice(h * H, (h + n) * H)
+            nc.sync.dma_start(out=out[i * P : (i + 1) * P, cols], in_=l_out[i][:, cols])
 
-        def sens_half(g, a):
-            for t in (2 * a, 2 * a + 1):
-                sens_transpose(g, t)
-                sens_copy(g, t)
-            sens_quantise(g, a)
+        steps = {}
 
-        def shocks_all(g, h, c):
-            shocks_interleave(g, h, c)
-            shocks_quantise(g, h)
+        def at(step, fn, *args):
+            steps.setdefault(step, []).append((fn, args))
 
-        def vq(g, h, c):
-            v_interleave(g, h, c)
-            v_quantise(g, h)
+        def sens_step(g, t):
+            if g == 0:
+                return 4 * (t // 2) - 8
+            return 3 + 39 * (2 * (g - 1) + t // 2) // 10
 
-        def ys(g, h):
-            for t in range(T):
-                y_product(g, t, h)
-                y_square(g, t, h)
-                v_clip(g, t, h, 1)
+        def y_step(g, t, h):
+            return 8 * g + (2 * t + h if g in WIDE else 4 * h + t)
 
-        def yw(g):
-            for t in range(T):
-                for h in range(2):
-                    y_product(g, t, h)
-                    y_square(g, t, h)
-                v_clip(g, t, 0, 2)
+        def short_step(i):
+            return 11 + 7 * i
 
-        def short_rest(i):
-            short_transpose(i, 0)
-            short_copy(i, 0)
-            short_transpose(i, 1)
-            short_copy(i, 1)
-            short_quantise(i)
+        def v_step(g, h):
+            if g in WIDE:
+                return y_step(g, T - 1, 1) + 6 + 4 * h
+            return y_step(g, T - 1, h) + 4
 
-        def loss_early(i, h):
-            loss_product(i, h, 0, 3)
-
-        def loss_late(i, h, on_vector):
-            loss_product(i, h, 3, 4)
-            loss_copy(i, h, on_vector)
-
-        def loss(i, h, on_vector):
-            loss_product(i, h, 0, 4)
-            loss_copy(i, h, on_vector)
-
-        sens_half(0,0)
-        shocks_all(0,0,512)
-        shocks_all(1,0,384)
-        small_constants()
-        sens_half(0,1)
-        ys(0,0)
-        sens_half(1,0)
-        shocks_all(0,1,320)
-        shocks_all(1,1,256)
-        vq(0,0,512)
-        ys(0,1)
-        sens_half(1,1)
-        vq(0,1,512)
-        yw(1)
-        sens_half(2,0)
-        vq(1,0,448)
-        sens_half(2,1)
-        vq(1,1,448)
-        yw(2)
-        sens_half(3,0)
-        vq(2,0,448)
-        sens_half(3,1)
-        vq(2,1,448)
-        yw(3)
-        vq(3,0,384)
-        vq(3,1,320)
-        short_widen(0)
-        short_rest(0)
-        short_widen(1)
-        short_rest(1)
+        every_y = [(g, t, h) for g in range(GN) for t in range(T) for h in range(2)]
+        at(-9, small_constants)
+        for g in range(GF):
+            for h in range(2):
+                at(2 * g - 8 if h == 0 else 1, shocks_interleave, g, h, 384)
+        for i in range(2):
+            for h in (1, 0):
+                at(49 + 56 * i, loss_product, i, h, 0, 3)
         for i in range(2):
             for h in range(2):
-                loss_early(i,h)
-        for i in range(2):
+                at(125 + i, loss_product, i, h, 3, 1)
+        for g, t, h in every_y:
+            at(y_step(g, t, h), y_product, g, t, h)
+        for g in range(GN):
+            for t in range(T):
+                at(sens_step(g, t), sens_transpose, g, t)
+        for i in range(3):
+            for half in range(2):
+                at(short_step(i) + 14, short_transpose, i, half)
+        for g, t, h in every_y:
+            at(y_step(g, t, h) + 0, y_square, g, t, h)
+        for g in range(GN):
+            for t in range(T):
+                at(sens_step(g, t) + (1 if g == 0 else 0), sens_copy, g, t)
+        for i in range(3):
+            for half in range(2):
+                at(short_step(i) + 15, short_copy, i, half)
+        for g, t, h in every_y:
+            if g not in WIDE:
+                at(y_step(g, t, h) + 2, v_clip, g, t, h, 1)
+            elif h == 1:
+                at(y_step(g, t, h) + 4, v_clip, g, t, 0, 2)
+        for g in range(GF):
             for h in range(2):
-                loss_late(i,h,False)
-            loss_store(i)
-        short_widen(2)
-        short_rest(2)
-        for i in range(2,NB):
-            if i+1<NB:
-                short_widen(i+1)
-            loss(i,0,False)
-            if i+1<NB:
-                short_rest(i+1)
-            loss(i,1,i==NB-1)
-            loss_store(i)
+                at(2 * g - 7 if h == 0 else 2, shocks_quantise, g, h)
+        for g in range(GN):
+            for half in range(2):
+                at(sens_step(g, 2 * half) + (2 if g == 0 else 2), sens_quantise, g, half)
+        for g in range(GN):
+            for h in range(2):
+                at(v_step(g, h) + 3, v_quantise, g, h)
+        for i in range(2):
+            at(short_step(i) + 19, short_quantise, i)
+        for g in range(GN):
+            for h in range(2):
+                at(v_step(g, h), v_interleave, g, h, 0 if (g, h) in ((1, 1), (3, 1)) else 128 if (g, h) == (3, 0) else H)
+        for i in range(3):
+            at(short_step(i), short_widen, i)
+
+        for step in sorted(steps):
+            for fn, args in steps[step]:
+                fn(*args)
+
+        for i in range(NB):
+            if i + 3 < NB:
+                short_widen(i + 3)
+            if i + 2 < NB:
+                short_quantise(i + 2)
+            loss_copy(i, 1, i == NB - 1)
+            if i == NB - 1:
+                loss_store(i, 1, 1)
+            if i + 3 < NB:
+                short_transpose(i + 3, 0)
+                short_transpose(i + 3, 1)
+            loss_copy(i, 0, False)
+            if i < NB - 1:
+                loss_store(i, 0, 2)
+            else:
+                loss_store(i, 0, 1)
+            if i + 2 < NB:
+                loss_product(i + 2, 1, 0, 4)
+                loss_product(i + 2, 0, 0, 4)
+            if i + 3 < NB:
+                short_copy(i + 3, 0)
+                short_copy(i + 3, 1)

@@ -23,6 +23,7 @@ GN = N // KP
 H = 512
 NB = B // P
 WIDE = (1, 2)
+SHARE = {(1, 1): 0, (2, 0): 384, (2, 1): 384, (3, 0): 384, (3, 1): 0}
 
 
 def tile_scenario_delta_gamma_losses_s7_kernel(tc, sens, shocks, tilt, cap, short_bytes, short_scale, out):
@@ -30,7 +31,7 @@ def tile_scenario_delta_gamma_losses_s7_kernel(tc, sens, shocks, tilt, cap, shor
     with ExitStack() as ctx:
         keep = ctx.enter_context(tc.tile_pool(name="keep", bufs=1))
         work = ctx.enter_context(tc.tile_pool(name="work", bufs=2))
-        psum = ctx.enter_context(tc.psum_pool(name="psum", bufs=3))
+        psum = ctx.enter_context(tc.psum_pool(name="psum", bufs=8))
 
         warm = keep.tile([P, 1], F32, name="warm")
         nc.vector.memset(warm[:], 0.0)
@@ -115,7 +116,7 @@ def tile_scenario_delta_gamma_losses_s7_kernel(tc, sens, shocks, tilt, cap, shor
         sens_codes = {}
 
         def sens_transpose(g, t):
-            bank = psum.tile([P, GF, 2, P], F32, name="tr")
+            bank = psum.tile([P, GF, 2, P], F32, name="bank")
             words = sens_raw[(g, t)].bitcast(F32)
             for q in range(GF):
                 for u in range(2):
@@ -130,8 +131,8 @@ def tile_scenario_delta_gamma_losses_s7_kernel(tc, sens, shocks, tilt, cap, shor
                            in_=sens_bank[(g, t)][:].rearrange("p q u m -> p q m u"))
 
         def sens_quantise(g, half):
-            codes = work.tile([P, 2, GF, P], U32, name="sens_codes", align_bytes=64, bufs=8)
-            scales = work.tile([P, 2, GF, P], U8, name="sens_scales", align_bytes=64, bufs=8)
+            codes = work.tile([P, 2, GF, P], U32, name="sens_codes", align_bytes=64, bufs=5)
+            scales = work.tile([P, 2, GF, P], U8, name="sens_scales", align_bytes=64, bufs=5)
             nc.vector.quantize_mx(out=codes[:].rearrange("p a q m -> p (a q m)").bitcast(X4),
                                   scales=scales[:].rearrange("p a q m -> p (a q m)"),
                                   in_=sens_grouped[(g, half)][:].rearrange("p a q m j -> p (a q m j)"))
@@ -145,7 +146,7 @@ def tile_scenario_delta_gamma_losses_s7_kernel(tc, sens, shocks, tilt, cap, shor
         def y_product(g, t, h):
             codes, scales = sens_codes[(g, t // 2)]
             cols = slice(h * H, (h + 1) * H)
-            bank = psum.tile([P, H], F32, name="acc", bufs=5)
+            bank = psum.tile([P, H], F32, name="bank")
             for q in range(GF):
                 nc.tensor.matmul_mx(out=bank[:], lhsT=codes[:, t % 2, q, :].bitcast(X4), lhsT_scale=scales[:, t % 2, q, :],
                                     rhs=sh_codes[:, q, cols].bitcast(X4), rhs_scale=sh_scales[:, q, cols],
@@ -192,13 +193,26 @@ def tile_scenario_delta_gamma_losses_s7_kernel(tc, sens, shocks, tilt, cap, shor
             nc.vector.tensor_tensor(out=wide[:], in0=bytes_t[:, i, :].bitcast(FP8), in1=scale_t[:], op=ALU.mult)
             st_wide[i] = wide
 
+        st_words = {}
+
+        def short_order(i, on_vector):
+            ordered = work.tile([P, GN, 2, P], F32, name="st_words", bufs=2)
+            words = st_wide[i][:].bitcast(F32).rearrange("p (q k u) -> p q u k", q=GN, u=2)
+            c = on_vector
+            if c > 0:
+                nc.vector.tensor_copy(out=ordered[:, 0:c], in_=words[:, 0:c])
+            if c < GN:
+                nc.scalar.copy(out=ordered[:, c:GN], in_=words[:, c:GN])
+            st_words[i] = ordered
+
         def short_transpose(i, half):
-            bank = psum.tile([P, 2, 2, P], F32, name="tr")
+            bank = psum.tile([P, 2, 2, P], F32, name="bank")
             words = st_wide[i][:].bitcast(F32)
             for q in range(2):
                 for u in range(2):
                     k0 = 256 * (2 * half + q)
-                    nc.tensor.transpose(bank[:, q, u, :], words[:, k0 + u : k0 + 256 : 2], ident[:])
+                    piece = st_words[i][:, 2 * half + q, u, :] if i in st_words else words[:, k0 + u : k0 + 256 : 2]
+                    nc.tensor.transpose(bank[:, q, u, :], piece, ident[:])
             st_bank[(i, half)] = bank
 
         def short_copy(i, half):
@@ -223,7 +237,7 @@ def tile_scenario_delta_gamma_losses_s7_kernel(tc, sens, shocks, tilt, cap, shor
             codes, scales = st_codes[i]
             cols = slice(h * H, (h + 1) * H)
             if g0 == 0:
-                l_bank[(i, h)] = psum.tile([P, H], F32, name="acc", bufs=5)
+                l_bank[(i, h)] = psum.tile([P, H], F32, name="bank")
             for g in range(g0, g0 + n):
                 nc.tensor.matmul_mx(out=l_bank[(i, h)][:], lhsT=codes[:, g, :].bitcast(X4), lhsT_scale=scales[:, g, :],
                                     rhs=v_codes[g][:, cols].bitcast(X4), rhs_scale=v_scales[g][:, cols],
@@ -250,7 +264,7 @@ def tile_scenario_delta_gamma_losses_s7_kernel(tc, sens, shocks, tilt, cap, shor
         def sens_step(g, t):
             if g == 0:
                 return 4 * (t // 2) - 8
-            return 3 + 39 * (2 * (g - 1) + t // 2) // 10
+            return 3 + 35 * (2 * (g - 1) + t // 2) // 10
 
         def y_step(g, t, h):
             return 8 * g + (2 * t + h if g in WIDE else 4 * h + t)
@@ -267,13 +281,7 @@ def tile_scenario_delta_gamma_losses_s7_kernel(tc, sens, shocks, tilt, cap, shor
         at(-9, small_constants)
         for g in range(GF):
             for h in range(2):
-                at(2 * g - 8 if h == 0 else 1, shocks_interleave, g, h, 384)
-        for i in range(2):
-            for h in (1, 0):
-                at(49 + 56 * i, loss_product, i, h, 0, 3)
-        for i in range(2):
-            for h in range(2):
-                at(125 + i, loss_product, i, h, 3, 1)
+                at(2 * g - 8 if h == 0 else -1, shocks_interleave, g, h, 384)
         for g, t, h in every_y:
             at(y_step(g, t, h), y_product, g, t, h)
         for g in range(GN):
@@ -281,7 +289,7 @@ def tile_scenario_delta_gamma_losses_s7_kernel(tc, sens, shocks, tilt, cap, shor
                 at(sens_step(g, t), sens_transpose, g, t)
         for i in range(3):
             for half in range(2):
-                at(short_step(i) + 14, short_transpose, i, half)
+                at(short_step(i) + 18, short_transpose, i, half)
         for g, t, h in every_y:
             at(y_step(g, t, h) + 0, y_square, g, t, h)
         for g in range(GN):
@@ -289,7 +297,7 @@ def tile_scenario_delta_gamma_losses_s7_kernel(tc, sens, shocks, tilt, cap, shor
                 at(sens_step(g, t) + (1 if g == 0 else 0), sens_copy, g, t)
         for i in range(3):
             for half in range(2):
-                at(short_step(i) + 15, short_copy, i, half)
+                at(short_step(i) + 20, short_copy, i, half)
         for g, t, h in every_y:
             if g not in WIDE:
                 at(y_step(g, t, h) + 2, v_clip, g, t, h, 1)
@@ -297,18 +305,18 @@ def tile_scenario_delta_gamma_losses_s7_kernel(tc, sens, shocks, tilt, cap, shor
                 at(y_step(g, t, h) + 4, v_clip, g, t, 0, 2)
         for g in range(GF):
             for h in range(2):
-                at(2 * g - 7 if h == 0 else 2, shocks_quantise, g, h)
+                at(2 * g - 7 if h == 0 else 1, shocks_quantise, g, h)
         for g in range(GN):
             for half in range(2):
                 at(sens_step(g, 2 * half) + (2 if g == 0 else 2), sens_quantise, g, half)
         for g in range(GN):
             for h in range(2):
-                at(v_step(g, h) + 3, v_quantise, g, h)
+                at(v_step(g, h) + 4, v_quantise, g, h)
         for i in range(2):
-            at(short_step(i) + 19, short_quantise, i)
+            at(short_step(i) + 24, short_quantise, i)
         for g in range(GN):
             for h in range(2):
-                at(v_step(g, h), v_interleave, g, h, 0 if (g, h) in ((1, 1), (3, 1)) else 128 if (g, h) == (3, 0) else H)
+                at(v_step(g, h), v_interleave, g, h, SHARE.get((g, h), H))
         for i in range(3):
             at(short_step(i), short_widen, i)
 
@@ -316,25 +324,31 @@ def tile_scenario_delta_gamma_losses_s7_kernel(tc, sens, shocks, tilt, cap, shor
             for fn, args in steps[step]:
                 fn(*args)
 
-        for i in range(NB):
+        for i, h, g0, n in ((0, 0, 0, 3), (0, 1, 0, 3), (0, 1, 3, 1), (1, 0, 0, 3),
+                            (1, 1, 0, 3), (1, 1, 3, 1), (0, 0, 3, 1), (1, 0, 3, 1)):
+            loss_product(i, h, g0, n)
+        for i in range(NB + 1):
+            if 4 <= i + 2 < NB:
+                short_order(i + 2, 2)
+            if 2 <= i < NB:
+                loss_product(i, 0, 0, 4)
+                loss_product(i, 1, 0, 4)
             if i + 3 < NB:
                 short_widen(i + 3)
+            if 3 <= i + 2 < NB:
+                short_transpose(i + 2, 0)
+                short_transpose(i + 2, 1)
+            if i > 0:
+                loss_copy(i - 1, 0, False)
+                if i == NB:
+                    loss_store(i - 1, 0, 1)
+                loss_copy(i - 1, 1, i == NB)
+                if i == NB:
+                    loss_store(i - 1, 1, 1)
+                else:
+                    loss_store(i - 1, 0, 2)
+            if 3 <= i + 2 < NB:
+                short_copy(i + 2, 0)
+                short_copy(i + 2, 1)
             if i + 2 < NB:
                 short_quantise(i + 2)
-            loss_copy(i, 1, i == NB - 1)
-            if i == NB - 1:
-                loss_store(i, 1, 1)
-            if i + 3 < NB:
-                short_transpose(i + 3, 0)
-                short_transpose(i + 3, 1)
-            loss_copy(i, 0, False)
-            if i < NB - 1:
-                loss_store(i, 0, 2)
-            else:
-                loss_store(i, 0, 1)
-            if i + 2 < NB:
-                loss_product(i + 2, 1, 0, 4)
-                loss_product(i + 2, 0, 0, 4)
-            if i + 3 < NB:
-                short_copy(i + 3, 0)
-                short_copy(i + 3, 1)

@@ -11,22 +11,29 @@ BF16 = mybir.dt.bfloat16
 U32 = mybir.dt.uint32
 U8 = mybir.dt.uint8
 FP8 = mybir.dt.float8_e4m3fn
-X4 = mybir.dt.float8_e4m3fn_x4
+FP8X4 = mybir.dt.float8_e4m3fn_x4
 ALU = mybir.AluOpType
 ACT = mybir.ActivationFunctionType
 
 P = 128
-T = 4
-KP = P * T
-GF = F // KP
-GN = N // KP
-H = 512
-NB = B // P
-WIDE = (1, 2)
-SHARE = {(1, 1): 0, (2, 0): 384, (2, 1): 384, (3, 0): 384, (3, 1): 0}
+PACK = 4
+K_PASS = P * PACK
+F_PASSES = F // K_PASS
+GROUPS = N // K_PASS
+HALF = S // 2
+BOOK_TILES = B // P
+
+SHOCKS_SHARE = 384
+V_SHARE = {(1, 1): 0, (2, 0): 384, (2, 1): 384, (3, 0): 384, (3, 1): 0}
+
+WIDE_GROUPS = (1, 2)
+
+ORDERED_TILES = (5, 6, 7)
 
 
-def tile_scenario_delta_gamma_losses_s7_kernel(tc, sens, shocks, tilt, cap, short_bytes, short_scale, out):
+def tile_scenario_delta_gamma_losses_s7_kernel(
+    tc, sens, shocks, tilt, cap, short_bytes, short_scale, out
+):
     nc = tc.nc
     with ExitStack() as ctx:
         keep = ctx.enter_context(tc.tile_pool(name="keep", bufs=1))
@@ -39,35 +46,42 @@ def tile_scenario_delta_gamma_losses_s7_kernel(tc, sens, shocks, tilt, cap, shor
         ident = keep.tile([P, P], F32, name="ident")
         make_identity(nc, ident[:])
 
-        tilt_bf = keep.tile([P, GN, 16], BF16, name="tilt_bf")
-        cap_bf = keep.tile([P, GN, 16], BF16, name="cap_bf")
-        nc.scalar.dma_start(out=tilt_bf[:, :, 0:T], in_=tilt.rearrange("(g p t) -> p g t", p=P, t=T))
-        nc.scalar.dma_start(out=cap_bf[:, :, 0:T], in_=cap.rearrange("(g p t) -> p g t", p=P, t=T))
+        tilt_raw = keep.tile([P, GROUPS, 16], BF16, name="tilt_raw")
+        cap_raw = keep.tile([P, GROUPS, 16], BF16, name="cap_raw")
+        nc.scalar.dma_start(out=tilt_raw[:, :, 0:PACK], in_=tilt.rearrange("(g m t) -> m g t", m=P, t=PACK))
+        nc.scalar.dma_start(out=cap_raw[:, :, 0:PACK], in_=cap.rearrange("(g m t) -> m g t", m=P, t=PACK))
+        half_tilt = keep.tile([P, GROUPS, PACK], F32, name="half_tilt")
+        half_tilt_sq = keep.tile([P, GROUPS, PACK], F32, name="half_tilt_sq")
+        cap_f32 = keep.tile([P, GROUPS, PACK], F32, name="cap_f32")
 
-        half_tilt = keep.tile([P, GN, T], F32, name="half_tilt")
-        quarter_sq = keep.tile([P, GN, T], F32, name="quarter_sq")
-        cap_f = keep.tile([P, GN, T], F32, name="cap_f")
+        def row_constants():
+            nc.vector.tensor_scalar(
+                out=half_tilt[:], in0=tilt_raw[:, :, 0:PACK], scalar1=0.5, scalar2=None, op0=ALU.mult
+            )
+            nc.vector.tensor_copy(out=cap_f32[:], in_=cap_raw[:, :, 0:PACK])
+            nc.vector.tensor_tensor(out=half_tilt_sq[:], in0=half_tilt[:], in1=half_tilt[:], op=ALU.mult)
 
-        def small_constants():
-            nc.vector.tensor_scalar(out=half_tilt[:], in0=tilt_bf[:, :, 0:T], scalar1=0.5, scalar2=None, op0=ALU.mult)
-            nc.vector.tensor_copy(out=cap_f[:], in_=cap_bf[:, :, 0:T])
-            nc.vector.tensor_tensor(out=quarter_sq[:], in0=half_tilt[:], in1=half_tilt[:], op=ALU.mult)
-
-        sens_v = sens.rearrange("(g m t) k -> g m t k", m=P, t=T)
-        shocks_v = shocks.rearrange("(g p t) s -> g p t s", p=P, t=T)
-        sens_raw = {}
+        sens_view = sens.rearrange("(g m t) k -> g m t k", m=P, t=PACK)
+        shocks_view = shocks.rearrange("(g p t) s -> g p t s", p=P, t=PACK)
+        bytes_view = short_bytes.rearrange("(i p) k -> p i k", p=P)
+        sens_rows = {}
         shocks_raw = {}
+        bytes_sb = keep.tile([P, BOOK_TILES, N], U8, name="bytes_sb")
+        scale_sb = keep.tile([P, N], F32, name="scale_sb")
 
         def load_sens(g, t0, n):
-            raw = keep.tile([P, n, F], BF16, name="sens_raw_%d_%d" % (g, t0))
-            nc.sync.dma_start(out=raw[:], in_=sens_v[g][:, t0 : t0 + n, :])
+            rows = keep.tile([P, n, F], BF16, name="sens_rows_%d_%d" % (g, t0))
+            nc.sync.dma_start(out=rows[:], in_=sens_view[g][:, t0 : t0 + n, :])
             for t in range(n):
-                sens_raw[(g, t0 + t)] = raw[:, t, :]
+                sens_rows[(g, t0 + t)] = rows[:, t, :]
 
         def load_shocks(g, h):
-            raw = keep.tile([P, T, H], BF16, name="shocks_raw_%d_%d" % (g, h))
-            nc.sync.dma_start(out=raw[:], in_=shocks_v[g][:, :, h * H : (h + 1) * H])
+            raw = keep.tile([P, PACK, HALF], BF16, name="shocks_raw_%d_%d" % (g, h))
+            nc.sync.dma_start(out=raw[:], in_=shocks_view[g][:, :, h * HALF : (h + 1) * HALF])
             shocks_raw[(g, h)] = raw
+
+        def load_bytes(i0, i1):
+            nc.sync.dma_start(out=bytes_sb[:, i0:i1, :], in_=bytes_view[:, i0:i1, :])
 
         load_shocks(0, 0)
         load_sens(0, 0, 2)
@@ -76,279 +90,296 @@ def tile_scenario_delta_gamma_losses_s7_kernel(tc, sens, shocks, tilt, cap, shor
         load_shocks(0, 1)
         load_shocks(1, 1)
         load_sens(1, 0, 4)
-        bytes_t = keep.tile([P, NB, N], U8, name="bytes_t")
-        scale_t = keep.tile([P, N], F32, name="scale_t")
-        bytes_v = short_bytes.rearrange("(i p) k -> p i k", p=P)
         load_sens(2, 0, 4)
-        nc.sync.dma_start(out=scale_t[:], in_=short_scale.rearrange("o k -> (o k)").partition_broadcast(P))
-        nc.sync.dma_start(out=bytes_t[:, 0:2, :], in_=bytes_v[:, 0:2, :])
+        nc.sync.dma_start(out=scale_sb[:], in_=short_scale.rearrange("o k -> (o k)").partition_broadcast(P))
+        load_bytes(0, 2)
         load_sens(3, 0, 4)
-        nc.sync.dma_start(out=bytes_t[:, 2:5, :], in_=bytes_v[:, 2:5, :])
-        nc.sync.dma_start(out=bytes_t[:, 5:8, :], in_=bytes_v[:, 5:8, :])
+        load_bytes(2, 5)
+        load_bytes(5, 8)
 
         ctx.enter_context(tc.manual_schedule())
 
-        sh_codes = keep.tile([P, GF, S], U32, name="sh_codes", align_bytes=64)
-        sh_scales = keep.tile([P, GF, S], U8, name="sh_scales", align_bytes=64)
-        v_codes = [keep.tile([P, S], U32, name="v_codes_%d" % g, align_bytes=64) for g in range(GN)]
-        v_scales = [keep.tile([P, S], U8, name="v_scales_%d" % g, align_bytes=64) for g in range(GN)]
+        shocks_codes = keep.tile([P, F_PASSES, S], U32, name="shocks_codes", align_bytes=64)
+        shocks_scales = keep.tile([P, F_PASSES, S], U8, name="shocks_scales", align_bytes=64)
+        v_codes = [keep.tile([P, S], U32, name="v_codes_%d" % g, align_bytes=64) for g in range(GROUPS)]
+        v_scales = [keep.tile([P, S], U8, name="v_scales_%d" % g, align_bytes=64) for g in range(GROUPS)]
 
-        sh_grouped = {}
+        def half_cols(h):
+            return slice(h * HALF, (h + 1) * HALF)
 
-        def shocks_interleave(g, h, on_vector):
-            grouped = work.tile([P, H, T], BF16, name="sh_grouped", align_bytes=64)
-            src = shocks_raw[(g, h)][:].rearrange("p t (b c) -> p b t c", c=4)
-            dst = grouped[:].rearrange("p (b c) t -> p b t c", c=4)
-            c = on_vector // 4
-            if c > 0:
-                nc.vector.tensor_copy(out=dst[:, 0:c], in_=src[:, 0:c])
-            if c < H // 4:
-                nc.scalar.copy(out=dst[:, c:], in_=src[:, c:])
-            sh_grouped[(g, h)] = grouped
+        def interleave(dst, src, vector_cols):
+            d = dst.rearrange("p (b c) t -> p b t c", c=4)
+            s = src.rearrange("p t (b c) -> p b t c", c=4)
+            cut = vector_cols // 4
+            if cut > 0:
+                nc.vector.tensor_copy(out=d[:, 0:cut], in_=s[:, 0:cut])
+            if cut < HALF // 4:
+                nc.scalar.copy(out=d[:, cut:], in_=s[:, cut:])
+
+        shocks_grouped = {}
+
+        def shocks_interleave(g, h):
+            shocks_grouped[(g, h)] = work.tile([P, HALF, PACK], BF16, name="shocks_grouped", align_bytes=64)
+            interleave(shocks_grouped[(g, h)][:], shocks_raw[(g, h)][:], SHOCKS_SHARE)
 
         def shocks_quantise(g, h):
-            cols = slice(h * H, (h + 1) * H)
-            nc.vector.quantize_mx(out=sh_codes[:, g, cols].bitcast(X4), scales=sh_scales[:, g, cols],
-                                  in_=sh_grouped[(g, h)][:].rearrange("p n t -> p (n t)"))
+            nc.vector.quantize_mx(
+                out=shocks_codes[:, g, half_cols(h)].bitcast(FP8X4),
+                scales=shocks_scales[:, g, half_cols(h)],
+                in_=shocks_grouped[(g, h)][:].rearrange("p n t -> p (n t)"),
+            )
+
+        def copy_words_out(dst, bank):
+            words = dst.rearrange("p q m j -> p (q m j)").bitcast(F32)
+            nc.scalar.copy(
+                out=words.rearrange("p (q m u) -> p q m u", q=2, u=2),
+                in_=bank.rearrange("p q u m -> p q m u"),
+            )
 
         sens_bank = {}
         sens_grouped = {}
-        sens_codes = {}
+        sens_operand = {}
 
         def sens_transpose(g, t):
-            bank = psum.tile([P, GF, 2, P], F32, name="bank")
-            words = sens_raw[(g, t)].bitcast(F32)
-            for q in range(GF):
+            sens_bank[(g, t)] = psum.tile([P, F_PASSES, 2, P], F32, name="bank")
+            words = sens_rows[(g, t)].bitcast(F32)
+            for q in range(F_PASSES):
                 for u in range(2):
-                    nc.tensor.transpose(bank[:, q, u, :], words[:, 256 * q + u : 256 * (q + 1) : 2], ident[:])
-            sens_bank[(g, t)] = bank
+                    nc.tensor.transpose(
+                        sens_bank[(g, t)][:, q, u, :], words[:, 256 * q + u : 256 * (q + 1) : 2], ident[:]
+                    )
 
         def sens_copy(g, t):
             if t % 2 == 0:
-                sens_grouped[(g, t // 2)] = work.tile([P, 2, GF, P, T], BF16, name="sens_grouped", align_bytes=64)
-            dst = sens_grouped[(g, t // 2)][:, t % 2].rearrange("p q m j -> p (q m j)").bitcast(F32)
-            nc.scalar.copy(out=dst.rearrange("p (q m u) -> p q m u", q=GF, u=2),
-                           in_=sens_bank[(g, t)][:].rearrange("p q u m -> p q m u"))
+                sens_grouped[(g, t // 2)] = work.tile(
+                    [P, 2, F_PASSES, P, PACK], BF16, name="sens_grouped", align_bytes=64
+                )
+            copy_words_out(sens_grouped[(g, t // 2)][:, t % 2], sens_bank[(g, t)][:])
 
-        def sens_quantise(g, half):
-            codes = work.tile([P, 2, GF, P], U32, name="sens_codes", align_bytes=64, bufs=5)
-            scales = work.tile([P, 2, GF, P], U8, name="sens_scales", align_bytes=64, bufs=5)
-            nc.vector.quantize_mx(out=codes[:].rearrange("p a q m -> p (a q m)").bitcast(X4),
-                                  scales=scales[:].rearrange("p a q m -> p (a q m)"),
-                                  in_=sens_grouped[(g, half)][:].rearrange("p a q m j -> p (a q m j)"))
-            sens_codes[(g, half)] = (codes, scales)
+        def sens_quantise(g, pair):
+            codes = work.tile([P, 2, F_PASSES, P], U32, name="sens_codes", align_bytes=64, bufs=5)
+            scales = work.tile([P, 2, F_PASSES, P], U8, name="sens_scales", align_bytes=64, bufs=5)
+            nc.vector.quantize_mx(
+                out=codes[:].rearrange("p a q m -> p (a q m)").bitcast(FP8X4),
+                scales=scales[:].rearrange("p a q m -> p (a q m)"),
+                in_=sens_grouped[(g, pair)][:].rearrange("p a q m j -> p (a q m j)"),
+            )
+            sens_operand[(g, pair)] = (codes, scales)
 
-        v_sq = {}
-        v_flat = {}
-        v_grouped = {}
         y_bank = {}
+        squares = {}
+        v_rows = {}
+        v_grouped = {}
 
         def y_product(g, t, h):
-            codes, scales = sens_codes[(g, t // 2)]
-            cols = slice(h * H, (h + 1) * H)
-            bank = psum.tile([P, H], F32, name="bank")
-            for q in range(GF):
-                nc.tensor.matmul_mx(out=bank[:], lhsT=codes[:, t % 2, q, :].bitcast(X4), lhsT_scale=scales[:, t % 2, q, :],
-                                    rhs=sh_codes[:, q, cols].bitcast(X4), rhs_scale=sh_scales[:, q, cols],
-                                    start=(q == 0), stop=(q == GF - 1))
-            y_bank[(g, t, h)] = bank
+            codes, scales = sens_operand[(g, t // 2)]
+            y_bank[(g, t, h)] = psum.tile([P, HALF], F32, name="bank")
+            for q in range(F_PASSES):
+                nc.tensor.matmul_mx(
+                    out=y_bank[(g, t, h)][:],
+                    lhsT=codes[:, t % 2, q, :].bitcast(FP8X4),
+                    lhsT_scale=scales[:, t % 2, q, :],
+                    rhs=shocks_codes[:, q, half_cols(h)].bitcast(FP8X4),
+                    rhs_scale=shocks_scales[:, q, half_cols(h)],
+                    start=(q == 0),
+                    stop=(q == F_PASSES - 1),
+                )
 
         def y_square(g, t, h):
-            if (g, t) not in v_sq:
-                v_sq[(g, t)] = work.tile([P, S], F32, name="v_sq", bufs=5)
-            nc.scalar.activation(out=v_sq[(g, t)][:, h * H : (h + 1) * H], in_=y_bank[(g, t, h)][:], func=ACT.Square,
-                                 bias=half_tilt[:, g, t : t + 1])
+            if (g, t) not in squares:
+                squares[(g, t)] = work.tile([P, S], F32, name="squares", bufs=5)
+            nc.scalar.activation(
+                out=squares[(g, t)][:, half_cols(h)],
+                in_=y_bank[(g, t, h)][:],
+                func=ACT.Square,
+                bias=half_tilt[:, g, t : t + 1],
+            )
 
-        def v_clip(g, t, h, n):
-            if g not in v_flat:
-                v_flat[g] = work.tile([P, T, S], BF16, name="v_flat", bufs=2)
-            cols = slice(h * H, (h + n) * H)
-            nc.vector.tensor_scalar(out=v_flat[g][:, t, cols], in0=v_sq[(g, t)][:, cols],
-                                    scalar1=quarter_sq[:, g, t : t + 1], scalar2=cap_f[:, g, t : t + 1],
-                                    op0=ALU.subtract, op1=ALU.min)
+        def v_clip(g, t, cols):
+            if g not in v_rows:
+                v_rows[g] = work.tile([P, PACK, S], BF16, name="v_rows")
+            nc.vector.tensor_scalar(
+                out=v_rows[g][:, t, cols],
+                in0=squares[(g, t)][:, cols],
+                scalar1=half_tilt_sq[:, g, t : t + 1],
+                scalar2=cap_f32[:, g, t : t + 1],
+                op0=ALU.subtract,
+                op1=ALU.min,
+            )
 
-        def v_interleave(g, h, on_vector):
-            grouped = work.tile([P, H, T], BF16, name="v_grouped", align_bytes=64, bufs=3)
-            src = v_flat[g][:, :, h * H : (h + 1) * H].rearrange("p t (b c) -> p b t c", c=4)
-            dst = grouped[:].rearrange("p (b c) t -> p b t c", c=4)
-            c = on_vector // 4
-            if c > 0:
-                nc.vector.tensor_copy(out=dst[:, 0:c], in_=src[:, 0:c])
-            if c < H // 4:
-                nc.scalar.copy(out=dst[:, c:], in_=src[:, c:])
-            v_grouped[(g, h)] = grouped
+        def v_interleave(g, h):
+            v_grouped[(g, h)] = work.tile([P, HALF, PACK], BF16, name="v_grouped", align_bytes=64, bufs=3)
+            interleave(v_grouped[(g, h)][:], v_rows[g][:, :, half_cols(h)], V_SHARE.get((g, h), HALF))
 
         def v_quantise(g, h):
-            cols = slice(h * H, (h + 1) * H)
-            nc.vector.quantize_mx(out=v_codes[g][:, cols].bitcast(X4), scales=v_scales[g][:, cols],
-                                  in_=v_grouped[(g, h)][:].rearrange("p n t -> p (n t)"))
+            nc.vector.quantize_mx(
+                out=v_codes[g][:, half_cols(h)].bitcast(FP8X4),
+                scales=v_scales[g][:, half_cols(h)],
+                in_=v_grouped[(g, h)][:].rearrange("p n t -> p (n t)"),
+            )
 
-        st_wide = {}
-        st_bank = {}
-        st_grouped = {}
-        st_codes = {}
+        short_wide = {}
+        short_words = {}
+        short_bank = {}
+        short_grouped = {}
+        short_operand = {}
 
         def short_widen(i):
-            wide = work.tile([P, N], BF16, name="st_wide", bufs=3)
-            nc.vector.tensor_tensor(out=wide[:], in0=bytes_t[:, i, :].bitcast(FP8), in1=scale_t[:], op=ALU.mult)
-            st_wide[i] = wide
+            short_wide[i] = work.tile([P, N], BF16, name="short_wide", bufs=3)
+            nc.vector.tensor_tensor(
+                out=short_wide[i][:], in0=bytes_sb[:, i, :].bitcast(FP8), in1=scale_sb[:], op=ALU.mult
+            )
 
-        st_words = {}
+        def short_order(i):
+            short_words[i] = work.tile([P, GROUPS, 2, P], F32, name="short_words")
+            words = short_wide[i][:].bitcast(F32).rearrange("p (g k u) -> p g u k", g=GROUPS, u=2)
+            nc.vector.tensor_copy(out=short_words[i][:, 0:2], in_=words[:, 0:2])
+            nc.scalar.copy(out=short_words[i][:, 2:4], in_=words[:, 2:4])
 
-        def short_order(i, on_vector):
-            ordered = work.tile([P, GN, 2, P], F32, name="st_words", bufs=2)
-            words = st_wide[i][:].bitcast(F32).rearrange("p (q k u) -> p q u k", q=GN, u=2)
-            c = on_vector
-            if c > 0:
-                nc.vector.tensor_copy(out=ordered[:, 0:c], in_=words[:, 0:c])
-            if c < GN:
-                nc.scalar.copy(out=ordered[:, c:GN], in_=words[:, c:GN])
-            st_words[i] = ordered
+        def short_transpose(i):
+            for two in range(GROUPS // 2):
+                bank = psum.tile([P, 2, 2, P], F32, name="bank")
+                words = short_wide[i][:].bitcast(F32)
+                for q in range(2):
+                    for u in range(2):
+                        g = 2 * two + q
+                        if i in ORDERED_TILES:
+                            piece = short_words[i][:, g, u, :]
+                        else:
+                            piece = words[:, 256 * g + u : 256 * (g + 1) : 2]
+                        nc.tensor.transpose(bank[:, q, u, :], piece, ident[:])
+                short_bank[(i, two)] = bank
 
-        def short_transpose(i, half):
-            bank = psum.tile([P, 2, 2, P], F32, name="bank")
-            words = st_wide[i][:].bitcast(F32)
-            for q in range(2):
-                for u in range(2):
-                    k0 = 256 * (2 * half + q)
-                    piece = st_words[i][:, 2 * half + q, u, :] if i in st_words else words[:, k0 + u : k0 + 256 : 2]
-                    nc.tensor.transpose(bank[:, q, u, :], piece, ident[:])
-            st_bank[(i, half)] = bank
-
-        def short_copy(i, half):
-            if half == 0:
-                st_grouped[i] = work.tile([P, GN, P, T], BF16, name="st_grouped", align_bytes=64)
-            dst = st_grouped[i][:, 2 * half : 2 * half + 2].rearrange("p q m j -> p (q m j)").bitcast(F32)
-            nc.scalar.copy(out=dst.rearrange("p (q m u) -> p q m u", q=2, u=2),
-                           in_=st_bank[(i, half)][:].rearrange("p q u m -> p q m u"))
+        def short_copy(i):
+            short_grouped[i] = work.tile([P, GROUPS, P, PACK], BF16, name="short_grouped", align_bytes=64)
+            for two in range(GROUPS // 2):
+                copy_words_out(short_grouped[i][:, 2 * two : 2 * two + 2], short_bank[(i, two)][:])
 
         def short_quantise(i):
-            codes = work.tile([P, GN, P], U32, name="st_codes", align_bytes=64, bufs=3)
-            scales = work.tile([P, GN, P], U8, name="st_scales", align_bytes=64, bufs=3)
-            nc.vector.quantize_mx(out=codes[:].rearrange("p q m -> p (q m)").bitcast(X4),
-                                  scales=scales[:].rearrange("p q m -> p (q m)"),
-                                  in_=st_grouped[i][:].rearrange("p q m j -> p (q m j)"))
-            st_codes[i] = (codes, scales)
+            codes = work.tile([P, GROUPS, P], U32, name="short_codes", align_bytes=64, bufs=3)
+            scales = work.tile([P, GROUPS, P], U8, name="short_scales", align_bytes=64, bufs=3)
+            nc.vector.quantize_mx(
+                out=codes[:].rearrange("p g m -> p (g m)").bitcast(FP8X4),
+                scales=scales[:].rearrange("p g m -> p (g m)"),
+                in_=short_grouped[i][:].rearrange("p g m j -> p (g m j)"),
+            )
+            short_operand[i] = (codes, scales)
 
-        l_bank = {}
-        l_out = {}
+        loss_bank = {}
+        loss_rows = {}
 
-        def loss_product(i, h, g0, n):
-            codes, scales = st_codes[i]
-            cols = slice(h * H, (h + 1) * H)
+        def loss_product(i, h, g0, g1):
+            codes, scales = short_operand[i]
             if g0 == 0:
-                l_bank[(i, h)] = psum.tile([P, H], F32, name="bank")
-            for g in range(g0, g0 + n):
-                nc.tensor.matmul_mx(out=l_bank[(i, h)][:], lhsT=codes[:, g, :].bitcast(X4), lhsT_scale=scales[:, g, :],
-                                    rhs=v_codes[g][:, cols].bitcast(X4), rhs_scale=v_scales[g][:, cols],
-                                    start=(g == 0), stop=(g == GN - 1))
+                loss_bank[(i, h)] = psum.tile([P, HALF], F32, name="bank")
+            for g in range(g0, g1):
+                nc.tensor.matmul_mx(
+                    out=loss_bank[(i, h)][:],
+                    lhsT=codes[:, g, :].bitcast(FP8X4),
+                    lhsT_scale=scales[:, g, :],
+                    rhs=v_codes[g][:, half_cols(h)].bitcast(FP8X4),
+                    rhs_scale=v_scales[g][:, half_cols(h)],
+                    start=(g == 0),
+                    stop=(g == GROUPS - 1),
+                )
 
-        def loss_copy(i, h, on_vector):
-            if i not in l_out:
-                l_out[i] = work.tile([P, S], F32, name="l_out", bufs=3)
-            dst = l_out[i][:, h * H : (h + 1) * H]
-            if on_vector:
-                nc.vector.tensor_copy(out=dst, in_=l_bank[(i, h)][:])
+        def loss_copy(i, h):
+            if h == 0:
+                loss_rows[i] = work.tile([P, S], F32, name="loss_rows", bufs=3)
+            if (i, h) == (BOOK_TILES - 1, 1):
+                nc.vector.tensor_copy(out=loss_rows[i][:, half_cols(h)], in_=loss_bank[(i, h)][:])
             else:
-                nc.scalar.copy(out=dst, in_=l_bank[(i, h)][:])
+                nc.scalar.copy(out=loss_rows[i][:, half_cols(h)], in_=loss_bank[(i, h)][:])
 
-        def loss_store(i, h, n):
-            cols = slice(h * H, (h + n) * H)
-            nc.sync.dma_start(out=out[i * P : (i + 1) * P, cols], in_=l_out[i][:, cols])
+        def loss_store(i, cols):
+            nc.sync.dma_start(out=out[i * P : (i + 1) * P, cols], in_=loss_rows[i][:, cols])
 
-        steps = {}
+        calls = {}
 
         def at(step, fn, *args):
-            steps.setdefault(step, []).append((fn, args))
-
-        def sens_step(g, t):
-            if g == 0:
-                return 4 * (t // 2) - 8
-            return 3 + 35 * (2 * (g - 1) + t // 2) // 10
+            calls.setdefault(step, []).append((fn, args))
 
         def y_step(g, t, h):
-            return 8 * g + (2 * t + h if g in WIDE else 4 * h + t)
+            return 8 * g + (2 * t + h if g in WIDE_GROUPS else 4 * h + t)
 
-        def short_step(i):
-            return 11 + 7 * i
+        def sens_step(g, pair):
+            if g == 0:
+                return 4 * pair - 8
+            return 3 + 7 * (2 * (g - 1) + pair) // 2
 
         def v_step(g, h):
-            if g in WIDE:
-                return y_step(g, T - 1, 1) + 6 + 4 * h
-            return y_step(g, T - 1, h) + 4
+            if g in WIDE_GROUPS:
+                return y_step(g, PACK - 1, 1) + 6 + 4 * h
+            return y_step(g, PACK - 1, h) + 4
 
-        every_y = [(g, t, h) for g in range(GN) for t in range(T) for h in range(2)]
-        at(-9, small_constants)
-        for g in range(GF):
-            for h in range(2):
-                at(2 * g - 8 if h == 0 else -1, shocks_interleave, g, h, 384)
-        for g, t, h in every_y:
+        pairs = [(g, pair) for g in range(GROUPS) for pair in range(2)]
+        halves = [(g, h) for g in range(GROUPS) for h in range(2)]
+        banks = [(g, t, h) for g in range(GROUPS) for t in range(PACK) for h in range(2)]
+
+        at(-9, row_constants)
+        for g in range(F_PASSES):
+            at(2 * g - 8, shocks_interleave, g, 0)
+            at(-1, shocks_interleave, g, 1)
+        for g, t, h in banks:
             at(y_step(g, t, h), y_product, g, t, h)
-        for g in range(GN):
-            for t in range(T):
-                at(sens_step(g, t), sens_transpose, g, t)
-        for i in range(3):
-            for half in range(2):
-                at(short_step(i) + 18, short_transpose, i, half)
-        for g, t, h in every_y:
-            at(y_step(g, t, h) + 0, y_square, g, t, h)
-        for g in range(GN):
-            for t in range(T):
-                at(sens_step(g, t) + (1 if g == 0 else 0), sens_copy, g, t)
-        for i in range(3):
-            for half in range(2):
-                at(short_step(i) + 20, short_copy, i, half)
-        for g, t, h in every_y:
-            if g not in WIDE:
-                at(y_step(g, t, h) + 2, v_clip, g, t, h, 1)
+        for g, pair in pairs:
+            for t in (2 * pair, 2 * pair + 1):
+                at(sens_step(g, pair), sens_transpose, g, t)
+        for i, step in enumerate((29, 32, 33)):
+            at(step, short_transpose, i)
+        for g, t, h in banks:
+            at(y_step(g, t, h), y_square, g, t, h)
+        for g, pair in pairs:
+            for t in (2 * pair, 2 * pair + 1):
+                at(sens_step(g, pair) + (1 if g == 0 else 0), sens_copy, g, t)
+        for i, step in enumerate((31, 34, 38)):
+            at(step, short_copy, i)
+        for g, t, h in banks:
+            if g not in WIDE_GROUPS:
+                at(y_step(g, t, h) + 2, v_clip, g, t, half_cols(h))
             elif h == 1:
-                at(y_step(g, t, h) + 4, v_clip, g, t, 0, 2)
-        for g in range(GF):
-            for h in range(2):
-                at(2 * g - 7 if h == 0 else 1, shocks_quantise, g, h)
-        for g in range(GN):
-            for half in range(2):
-                at(sens_step(g, 2 * half) + (2 if g == 0 else 2), sens_quantise, g, half)
-        for g in range(GN):
-            for h in range(2):
-                at(v_step(g, h) + 4, v_quantise, g, h)
-        for i in range(2):
-            at(short_step(i) + 24, short_quantise, i)
-        for g in range(GN):
-            for h in range(2):
-                at(v_step(g, h), v_interleave, g, h, SHARE.get((g, h), H))
+                at(y_step(g, t, h) + 4, v_clip, g, t, slice(0, S))
+        for g in range(F_PASSES):
+            at(2 * g - 7, shocks_quantise, g, 0)
+            at(1, shocks_quantise, g, 1)
+        for g, pair in pairs:
+            at(sens_step(g, pair) + 2, sens_quantise, g, pair)
+        for i, step in enumerate((33, 36)):
+            at(step, short_quantise, i)
+        for g, h in halves:
+            at(v_step(g, h) + 4, v_quantise, g, h)
+        for g, h in halves:
+            at(v_step(g, h), v_interleave, g, h)
         for i in range(3):
-            at(short_step(i), short_widen, i)
+            at(11 + 7 * i, short_widen, i)
 
-        for step in sorted(steps):
-            for fn, args in steps[step]:
+        for step in sorted(calls):
+            for fn, args in calls[step]:
                 fn(*args)
 
-        for i, h, g0, n in ((0, 0, 0, 3), (0, 1, 0, 3), (0, 1, 3, 1), (1, 0, 0, 3),
-                            (1, 1, 0, 3), (1, 1, 3, 1), (0, 0, 3, 1), (1, 0, 3, 1)):
-            loss_product(i, h, g0, n)
-        for i in range(NB + 1):
-            if 4 <= i + 2 < NB:
-                short_order(i + 2, 2)
-            if 2 <= i < NB:
-                loss_product(i, 0, 0, 4)
-                loss_product(i, 1, 0, 4)
-            if i + 3 < NB:
+        for i, h, g0, g1 in (
+            (0, 0, 0, 2), (0, 1, 0, 2), (0, 0, 2, 4), (1, 0, 0, 4), (1, 1, 0, 2), (0, 1, 2, 4), (1, 1, 2, 4)
+        ):
+            loss_product(i, h, g0, g1)
+        for i in range(BOOK_TILES + 1):
+            if i + 2 in ORDERED_TILES:
+                short_order(i + 2)
+            if 2 <= i < BOOK_TILES:
+                loss_product(i, 0, 0, GROUPS)
+                loss_product(i, 1, 0, GROUPS)
+            if i + 3 < BOOK_TILES:
                 short_widen(i + 3)
-            if 3 <= i + 2 < NB:
-                short_transpose(i + 2, 0)
-                short_transpose(i + 2, 1)
-            if i > 0:
-                loss_copy(i - 1, 0, False)
-                if i == NB:
-                    loss_store(i - 1, 0, 1)
-                loss_copy(i - 1, 1, i == NB)
-                if i == NB:
-                    loss_store(i - 1, 1, 1)
-                else:
-                    loss_store(i - 1, 0, 2)
-            if 3 <= i + 2 < NB:
-                short_copy(i + 2, 0)
-                short_copy(i + 2, 1)
-            if i + 2 < NB:
+            if 1 <= i < BOOK_TILES - 2:
+                short_transpose(i + 2)
+            if 1 <= i < BOOK_TILES:
+                loss_copy(i - 1, 0)
+                loss_copy(i - 1, 1)
+                loss_store(i - 1, slice(0, S))
+            if i == BOOK_TILES:
+                for h in range(2):
+                    loss_copy(i - 1, h)
+                    loss_store(i - 1, half_cols(h))
+            if 1 <= i < BOOK_TILES - 2:
+                short_copy(i + 2)
+            if i + 2 < BOOK_TILES:
                 short_quantise(i + 2)

from contextlib import ExitStack

import concourse.mybir as mybir
from concourse.masks import make_identity

N, F, S, B = 2048, 1024, 1024, 1024
FLOPS = 2 * N * F * S + 2 * B * N * S

F32 = mybir.dt.float32
BF16 = mybir.dt.bfloat16
U32 = mybir.dt.uint32
U8 = mybir.dt.uint8
FP8 = mybir.dt.float8_e4m3fn
FP8X4 = mybir.dt.float8_e4m3fn_x4
ALU = mybir.AluOpType
ACT = mybir.ActivationFunctionType

P = 128
PACK = 4
K_PASS = P * PACK
F_PASSES = F // K_PASS
GROUPS = N // K_PASS
HALF = S // 2
BOOK_TILES = B // P

SHOCKS_SHARE = 384
V_SHARE = {(1, 1): 0, (2, 0): 384, (2, 1): 384, (3, 0): 384, (3, 1): 0}

WIDE_GROUPS = (1, 2)

ORDERED_TILES = (5, 6, 7)


def tile_scenario_delta_gamma_losses_s7_kernel(
    tc, sens, shocks, tilt, cap, short_bytes, short_scale, out
):
    nc = tc.nc
    with ExitStack() as ctx:
        keep = ctx.enter_context(tc.tile_pool(name="keep", bufs=1))
        work = ctx.enter_context(tc.tile_pool(name="work", bufs=2))
        psum = ctx.enter_context(tc.psum_pool(name="psum", bufs=8))

        warm = keep.tile([P, 1], F32, name="warm")
        nc.vector.memset(warm[:], 0.0)
        nc.scalar.activation(out=warm[:], in_=warm[:], func=ACT.Square)
        ident = keep.tile([P, P], F32, name="ident")
        make_identity(nc, ident[:])

        tilt_raw = keep.tile([P, GROUPS, 16], BF16, name="tilt_raw")
        cap_raw = keep.tile([P, GROUPS, 16], BF16, name="cap_raw")
        nc.scalar.dma_start(out=tilt_raw[:, :, 0:PACK], in_=tilt.rearrange("(g m t) -> m g t", m=P, t=PACK))
        nc.scalar.dma_start(out=cap_raw[:, :, 0:PACK], in_=cap.rearrange("(g m t) -> m g t", m=P, t=PACK))
        half_tilt = keep.tile([P, GROUPS, PACK], F32, name="half_tilt")
        half_tilt_sq = keep.tile([P, GROUPS, PACK], F32, name="half_tilt_sq")
        cap_f32 = keep.tile([P, GROUPS, PACK], F32, name="cap_f32")

        def row_constants():
            nc.vector.tensor_scalar(
                out=half_tilt[:], in0=tilt_raw[:, :, 0:PACK], scalar1=0.5, scalar2=None, op0=ALU.mult
            )
            nc.vector.tensor_copy(out=cap_f32[:], in_=cap_raw[:, :, 0:PACK])
            nc.vector.tensor_tensor(out=half_tilt_sq[:], in0=half_tilt[:], in1=half_tilt[:], op=ALU.mult)

        sens_view = sens.rearrange("(g m t) k -> g m t k", m=P, t=PACK)
        shocks_view = shocks.rearrange("(g p t) s -> g p t s", p=P, t=PACK)
        bytes_view = short_bytes.rearrange("(i p) k -> p i k", p=P)
        sens_rows = {}
        shocks_raw = {}
        bytes_sb = keep.tile([P, BOOK_TILES, N], U8, name="bytes_sb")
        scale_sb = keep.tile([P, N], F32, name="scale_sb")

        def load_sens(g, t0, n):
            rows = keep.tile([P, n, F], BF16, name="sens_rows_%d_%d" % (g, t0))
            nc.sync.dma_start(out=rows[:], in_=sens_view[g][:, t0 : t0 + n, :])
            for t in range(n):
                sens_rows[(g, t0 + t)] = rows[:, t, :]

        def load_shocks(g, h):
            raw = keep.tile([P, PACK, HALF], BF16, name="shocks_raw_%d_%d" % (g, h))
            nc.sync.dma_start(out=raw[:], in_=shocks_view[g][:, :, h * HALF : (h + 1) * HALF])
            shocks_raw[(g, h)] = raw

        def load_bytes(i0, i1):
            nc.sync.dma_start(out=bytes_sb[:, i0:i1, :], in_=bytes_view[:, i0:i1, :])

        load_shocks(0, 0)
        load_sens(0, 0, 2)
        load_shocks(1, 0)
        load_sens(0, 2, 2)
        load_shocks(0, 1)
        load_shocks(1, 1)
        load_sens(1, 0, 4)
        load_sens(2, 0, 4)
        nc.sync.dma_start(out=scale_sb[:], in_=short_scale.rearrange("o k -> (o k)").partition_broadcast(P))
        load_bytes(0, 2)
        load_sens(3, 0, 4)
        load_bytes(2, 5)
        load_bytes(5, 8)

        ctx.enter_context(tc.manual_schedule())

        shocks_codes = keep.tile([P, F_PASSES, S], U32, name="shocks_codes", align_bytes=64)
        shocks_scales = keep.tile([P, F_PASSES, S], U8, name="shocks_scales", align_bytes=64)
        v_codes = [keep.tile([P, S], U32, name="v_codes_%d" % g, align_bytes=64) for g in range(GROUPS)]
        v_scales = [keep.tile([P, S], U8, name="v_scales_%d" % g, align_bytes=64) for g in range(GROUPS)]

        def half_cols(h):
            return slice(h * HALF, (h + 1) * HALF)

        def interleave(dst, src, vector_cols):
            d = dst.rearrange("p (b c) t -> p b t c", c=4)
            s = src.rearrange("p t (b c) -> p b t c", c=4)
            cut = vector_cols // 4
            if cut > 0:
                nc.vector.tensor_copy(out=d[:, 0:cut], in_=s[:, 0:cut])
            if cut < HALF // 4:
                nc.scalar.copy(out=d[:, cut:], in_=s[:, cut:])

        shocks_grouped = {}

        def shocks_interleave(g, h):
            shocks_grouped[(g, h)] = work.tile([P, HALF, PACK], BF16, name="shocks_grouped", align_bytes=64)
            interleave(shocks_grouped[(g, h)][:], shocks_raw[(g, h)][:], SHOCKS_SHARE)

        def shocks_quantise(g, h):
            nc.vector.quantize_mx(
                out=shocks_codes[:, g, half_cols(h)].bitcast(FP8X4),
                scales=shocks_scales[:, g, half_cols(h)],
                in_=shocks_grouped[(g, h)][:].rearrange("p n t -> p (n t)"),
            )

        def copy_words_out(dst, bank):
            words = dst.rearrange("p q m j -> p (q m j)").bitcast(F32)
            nc.scalar.copy(
                out=words.rearrange("p (q m u) -> p q m u", q=2, u=2),
                in_=bank.rearrange("p q u m -> p q m u"),
            )

        sens_bank = {}
        sens_grouped = {}
        sens_operand = {}

        def sens_transpose(g, t):
            sens_bank[(g, t)] = psum.tile([P, F_PASSES, 2, P], F32, name="bank")
            words = sens_rows[(g, t)].bitcast(F32)
            for q in range(F_PASSES):
                for u in range(2):
                    nc.tensor.transpose(
                        sens_bank[(g, t)][:, q, u, :], words[:, 256 * q + u : 256 * (q + 1) : 2], ident[:]
                    )

        def sens_copy(g, t):
            if t % 2 == 0:
                sens_grouped[(g, t // 2)] = work.tile(
                    [P, 2, F_PASSES, P, PACK], BF16, name="sens_grouped", align_bytes=64
                )
            copy_words_out(sens_grouped[(g, t // 2)][:, t % 2], sens_bank[(g, t)][:])

        def sens_quantise(g, pair):
            codes = work.tile([P, 2, F_PASSES, P], U32, name="sens_codes", align_bytes=64, bufs=5)
            scales = work.tile([P, 2, F_PASSES, P], U8, name="sens_scales", align_bytes=64, bufs=5)
            nc.vector.quantize_mx(
                out=codes[:].rearrange("p a q m -> p (a q m)").bitcast(FP8X4),
                scales=scales[:].rearrange("p a q m -> p (a q m)"),
                in_=sens_grouped[(g, pair)][:].rearrange("p a q m j -> p (a q m j)"),
            )
            sens_operand[(g, pair)] = (codes, scales)

        y_bank = {}
        squares = {}
        v_rows = {}
        v_grouped = {}

        def y_product(g, t, h):
            codes, scales = sens_operand[(g, t // 2)]
            y_bank[(g, t, h)] = psum.tile([P, HALF], F32, name="bank")
            for q in range(F_PASSES):
                nc.tensor.matmul_mx(
                    out=y_bank[(g, t, h)][:],
                    lhsT=codes[:, t % 2, q, :].bitcast(FP8X4),
                    lhsT_scale=scales[:, t % 2, q, :],
                    rhs=shocks_codes[:, q, half_cols(h)].bitcast(FP8X4),
                    rhs_scale=shocks_scales[:, q, half_cols(h)],
                    start=(q == 0),
                    stop=(q == F_PASSES - 1),
                )

        def y_square(g, t, h):
            if (g, t) not in squares:
                squares[(g, t)] = work.tile([P, S], F32, name="squares", bufs=5)
            nc.scalar.activation(
                out=squares[(g, t)][:, half_cols(h)],
                in_=y_bank[(g, t, h)][:],
                func=ACT.Square,
                bias=half_tilt[:, g, t : t + 1],
            )

        def v_clip(g, t, cols):
            if g not in v_rows:
                v_rows[g] = work.tile([P, PACK, S], BF16, name="v_rows")
            nc.vector.tensor_scalar(
                out=v_rows[g][:, t, cols],
                in0=squares[(g, t)][:, cols],
                scalar1=half_tilt_sq[:, g, t : t + 1],
                scalar2=cap_f32[:, g, t : t + 1],
                op0=ALU.subtract,
                op1=ALU.min,
            )

        def v_interleave(g, h):
            v_grouped[(g, h)] = work.tile([P, HALF, PACK], BF16, name="v_grouped", align_bytes=64, bufs=3)
            interleave(v_grouped[(g, h)][:], v_rows[g][:, :, half_cols(h)], V_SHARE.get((g, h), HALF))

        def v_quantise(g, h):
            nc.vector.quantize_mx(
                out=v_codes[g][:, half_cols(h)].bitcast(FP8X4),
                scales=v_scales[g][:, half_cols(h)],
                in_=v_grouped[(g, h)][:].rearrange("p n t -> p (n t)"),
            )

        short_wide = {}
        short_words = {}
        short_bank = {}
        short_grouped = {}
        short_operand = {}

        def short_widen(i):
            short_wide[i] = work.tile([P, N], BF16, name="short_wide", bufs=3)
            nc.vector.tensor_tensor(
                out=short_wide[i][:], in0=bytes_sb[:, i, :].bitcast(FP8), in1=scale_sb[:], op=ALU.mult
            )

        def short_order(i):
            short_words[i] = work.tile([P, GROUPS, 2, P], F32, name="short_words")
            words = short_wide[i][:].bitcast(F32).rearrange("p (g k u) -> p g u k", g=GROUPS, u=2)
            nc.vector.tensor_copy(out=short_words[i][:, 0:2], in_=words[:, 0:2])
            nc.scalar.copy(out=short_words[i][:, 2:4], in_=words[:, 2:4])

        def short_transpose(i):
            for two in range(GROUPS // 2):
                bank = psum.tile([P, 2, 2, P], F32, name="bank")
                words = short_wide[i][:].bitcast(F32)
                for q in range(2):
                    for u in range(2):
                        g = 2 * two + q
                        if i in ORDERED_TILES:
                            piece = short_words[i][:, g, u, :]
                        else:
                            piece = words[:, 256 * g + u : 256 * (g + 1) : 2]
                        nc.tensor.transpose(bank[:, q, u, :], piece, ident[:])
                short_bank[(i, two)] = bank

        def short_copy(i):
            short_grouped[i] = work.tile([P, GROUPS, P, PACK], BF16, name="short_grouped", align_bytes=64)
            for two in range(GROUPS // 2):
                copy_words_out(short_grouped[i][:, 2 * two : 2 * two + 2], short_bank[(i, two)][:])

        def short_quantise(i):
            codes = work.tile([P, GROUPS, P], U32, name="short_codes", align_bytes=64, bufs=3)
            scales = work.tile([P, GROUPS, P], U8, name="short_scales", align_bytes=64, bufs=3)
            nc.vector.quantize_mx(
                out=codes[:].rearrange("p g m -> p (g m)").bitcast(FP8X4),
                scales=scales[:].rearrange("p g m -> p (g m)"),
                in_=short_grouped[i][:].rearrange("p g m j -> p (g m j)"),
            )
            short_operand[i] = (codes, scales)

        loss_bank = {}
        loss_rows = {}

        def loss_product(i, h, g0, g1):
            codes, scales = short_operand[i]
            if g0 == 0:
                loss_bank[(i, h)] = psum.tile([P, HALF], F32, name="bank")
            for g in range(g0, g1):
                nc.tensor.matmul_mx(
                    out=loss_bank[(i, h)][:],
                    lhsT=codes[:, g, :].bitcast(FP8X4),
                    lhsT_scale=scales[:, g, :],
                    rhs=v_codes[g][:, half_cols(h)].bitcast(FP8X4),
                    rhs_scale=v_scales[g][:, half_cols(h)],
                    start=(g == 0),
                    stop=(g == GROUPS - 1),
                )

        def loss_copy(i, h):
            if h == 0:
                loss_rows[i] = work.tile([P, S], F32, name="loss_rows", bufs=3)
            if (i, h) == (BOOK_TILES - 1, 1):
                nc.vector.tensor_copy(out=loss_rows[i][:, half_cols(h)], in_=loss_bank[(i, h)][:])
            else:
                nc.scalar.copy(out=loss_rows[i][:, half_cols(h)], in_=loss_bank[(i, h)][:])

        def loss_store(i, cols):
            nc.sync.dma_start(out=out[i * P : (i + 1) * P, cols], in_=loss_rows[i][:, cols])

        calls = {}

        def at(step, fn, *args):
            calls.setdefault(step, []).append((fn, args))

        def y_step(g, t, h):
            return 8 * g + (2 * t + h if g in WIDE_GROUPS else 4 * h + t)

        def sens_step(g, pair):
            if g == 0:
                return 4 * pair - 8
            return 3 + 7 * (2 * (g - 1) + pair) // 2

        def v_step(g, h):
            if g in WIDE_GROUPS:
                return y_step(g, PACK - 1, 1) + 6 + 4 * h
            return y_step(g, PACK - 1, h) + 4

        pairs = [(g, pair) for g in range(GROUPS) for pair in range(2)]
        halves = [(g, h) for g in range(GROUPS) for h in range(2)]
        banks = [(g, t, h) for g in range(GROUPS) for t in range(PACK) for h in range(2)]

        at(-9, row_constants)
        for g in range(F_PASSES):
            at(2 * g - 8, shocks_interleave, g, 0)
            at(-1, shocks_interleave, g, 1)
        for g, t, h in banks:
            at(y_step(g, t, h), y_product, g, t, h)
        for g, pair in pairs:
            for t in (2 * pair, 2 * pair + 1):
                at(sens_step(g, pair), sens_transpose, g, t)
        for i, step in enumerate((29, 32, 33)):
            at(step, short_transpose, i)
        for g, t, h in banks:
            at(y_step(g, t, h), y_square, g, t, h)
        for g, pair in pairs:
            for t in (2 * pair, 2 * pair + 1):
                at(sens_step(g, pair) + (1 if g == 0 else 0), sens_copy, g, t)
        for i, step in enumerate((31, 34, 38)):
            at(step, short_copy, i)
        for g, t, h in banks:
            if g not in WIDE_GROUPS:
                at(y_step(g, t, h) + 2, v_clip, g, t, half_cols(h))
            elif h == 1:
                at(y_step(g, t, h) + 4, v_clip, g, t, slice(0, S))
        for g in range(F_PASSES):
            at(2 * g - 7, shocks_quantise, g, 0)
            at(1, shocks_quantise, g, 1)
        for g, pair in pairs:
            at(sens_step(g, pair) + 2, sens_quantise, g, pair)
        for i, step in enumerate((33, 36)):
            at(step, short_quantise, i)
        for g, h in halves:
            at(v_step(g, h) + 4, v_quantise, g, h)
        for g, h in halves:
            at(v_step(g, h), v_interleave, g, h)
        for i in range(3):
            at(11 + 7 * i, short_widen, i)

        for step in sorted(calls):
            for fn, args in calls[step]:
                fn(*args)

        for i, h, g0, g1 in (
            (0, 0, 0, 2), (0, 1, 0, 2), (0, 0, 2, 4), (1, 0, 0, 4), (1, 1, 0, 2), (0, 1, 2, 4), (1, 1, 2, 4)
        ):
            loss_product(i, h, g0, g1)
        for i in range(BOOK_TILES + 1):
            if i + 2 in ORDERED_TILES:
                short_order(i + 2)
            if 2 <= i < BOOK_TILES:
                loss_product(i, 0, 0, GROUPS)
                loss_product(i, 1, 0, GROUPS)
            if i + 3 < BOOK_TILES:
                short_widen(i + 3)
            if 1 <= i < BOOK_TILES - 2:
                short_transpose(i + 2)
            if 1 <= i < BOOK_TILES:
                loss_copy(i - 1, 0)
                loss_copy(i - 1, 1)
                loss_store(i - 1, slice(0, S))
            if i == BOOK_TILES:
                for h in range(2):
                    loss_copy(i - 1, h)
                    loss_store(i - 1, half_cols(h))
            if 1 <= i < BOOK_TILES - 2:
                short_copy(i + 2)
            if i + 2 < BOOK_TILES:
                short_quantise(i + 2)
